import numpy as np
import ml_dtypes


def mxq(x, axis, fmt="e4m3"):
    dtype, down = {"e4m3": (ml_dtypes.float8_e4m3fn, 7), "e5m2": (ml_dtypes.float8_e5m2, 14)}[fmt]
    v = np.moveaxis(np.asarray(x, np.float32).astype(ml_dtypes.bfloat16).astype(np.float64), axis, -1)
    blocks = v.reshape(v.shape[:-1] + (-1, 32))
    amax = np.abs(blocks).max(-1, keepdims=True)
    byte = np.maximum(np.where(amax > 0, np.frexp(amax)[1] - 1 + 127, 0) - down, 1)
    scale = np.exp2(byte - 127.0)
    codes = (blocks / scale).astype(np.float32).astype(dtype).astype(np.float64)
    return np.moveaxis((codes * scale).reshape(v.shape), -1, axis)


WIDE = False


def mx_kscale(k):
    if not WIDE:
        return np.ones(k)
    levels = np.array([10, -10, 5, -5, 0])
    if k % 512:
        return np.exp2(np.random.permutation(np.resize(levels, k // 32))).repeat(32)
    a = np.empty((k // 512, 16))
    for p in range(k // 512):
        a[p, :8] = np.random.permutation(np.resize(levels, 8))
        for g in range(8):
            far = levels[np.abs(levels - a[p, g]) >= 10]
            a[p, g + 8] = far[np.random.randint(len(far))]
    return np.exp2(a.ravel()).repeat(32)


def f64(x):
    return np.asarray(x).astype(np.float64)


def striped(idx):
    return np.tile(idx.reshape(-1, 16).T, (8, 1)).astype(np.uint16)


def unstriped(offs):
    return offs[:16].T.reshape(-1).astype(np.int64)


E2M1 = np.array([0.0, 0.5, 1.0, 1.5, 2.0, 3.0, 4.0, 6.0, -0.0, -0.5, -1.0, -1.5, -2.0, -3.0, -4.0, -6.0])


def pack_weight(w, fmt):
    k, n = w.shape
    w = f64(np.asarray(w, np.float32).astype(ml_dtypes.bfloat16)).reshape(k // 32, 32, n)
    amax = np.abs(w).max(1)
    if fmt == "e4m3":
        byte = np.frexp(amax)[1] - 1 + 127 - 7
    else:
        mant, ex = np.frexp(amax / 6.0)
        byte = np.where(mant > 0.5, ex, ex - 1) + 127
    byte = np.clip(np.where(amax > 0, byte, 1), 1, 254)
    scaled = (w * np.exp2(127.0 - byte)[:, None, :]).reshape(k, n).astype(np.float32)
    by_word = np.ascontiguousarray(scaled.reshape(k // 512, 128, 4, n).transpose(0, 1, 3, 2))
    if fmt == "e4m3":
        words = by_word.astype(ml_dtypes.float8_e4m3fn).view(np.uint8)
    else:
        c = by_word.astype(ml_dtypes.float4_e2m1fn).view(np.uint8) & 0xF
        words = (c[..., 0::2] | (c[..., 1::2] << 4)).reshape(k // 512, 128, 2 * n)
    return np.ascontiguousarray(words), np.ascontiguousarray(byte.astype(np.uint8).reshape(k // 512, 16, n))


def unpack_weight(words, scales, fmt):
    g, _, n = scales.shape
    words = np.ascontiguousarray(words).reshape(g, 128, n, -1)
    if fmt == "e4m3":
        vals = words.view(ml_dtypes.float8_e4m3fn).astype(np.float64)
    else:
        nib = np.empty((g, 128, n, 4), np.uint8)
        nib[..., 0::2] = words & 0xF
        nib[..., 1::2] = words >> 4
        vals = E2M1[nib]
    vals = vals * np.repeat(np.exp2(scales.astype(np.float64) - 127.0), 8, axis=1)[..., None]
    return vals.transpose(0, 1, 3, 2).reshape(g * 512, n)


def gelu(v):
    return 0.5 * v * (1.0 + np.tanh(np.sqrt(2.0 / np.pi) * (v + 0.044715 * v**3)))


K, H, T, S, P = 1024, 1024, 2048, 1024, 512

def setup_inputs():
    n = np.random.standard_normal
    s = mx_kscale(K)[:, None]
    u = mx_kscale(H)[:, None]
    tab_words, tab_scales = pack_weight(n((K, T)) * s, "e4m3")
    w4_words, w4_scales = pack_weight(0.5 * n((K, H)) / np.sqrt(K) / s, "e2m1")
    return {
        "tab_words": tab_words, "tab_scales": tab_scales,
        "offs": striped(np.random.permutation(T)[:S]),
        "w4_words": w4_words, "w4_scales": w4_scales,
        "pattern": n((H, S)).astype(np.float32),
        "gain": (np.exp(0.3 * n(H)) * u[:, 0]).astype(np.float32),
        "pos1": striped(np.random.permutation(S)[:P]),
        "light": np.exp(0.4 * n((H, P))).astype(np.float32),
        "w2": (2.0 * n((H, H)) / np.sqrt(H) / u).astype(np.float32),
        "skip": (1.5 * np.exp(0.3 * n(H)) / u[:, 0]).astype(np.float32),
        "wgo": np.exp(0.3 * n((128, P))).astype(np.float32),
    }

def reference(tab_words, tab_scales, offs, w4_words, w4_scales, pattern, gain, pos1, light, w2, skip, wgo):
    v = unpack_weight(tab_words, tab_scales, "e4m3")[:, unstriped(offs)]
    w4 = unpack_weight(w4_words, w4_scales, "e2m1")
    wave = np.sin(w4.T @ v)
    h = f64(gain)[:, None] * (wave * f64(pattern))
    x = h[:, unstriped(pos1)] * f64(light)
    y = mxq(f64(w2), 0, "e4m3").T @ mxq(x, 0, "e4m3")
    out = f64(skip)[:, None] * h
    y = np.maximum(y, out[:, unstriped(pos1)])
    out[:, unstriped(pos1)] = np.tile(f64(wgo), (H // 128, 1)) * y
    return out

@@ -1,0 +1,267 @@
+import math
+from contextlib import ExitStack
+
+import concourse.mybir as mybir
+from concourse.masks import make_identity
+
+K, H, T, S, M = 1024, 1024, 2048, 1024, 512
+FLOPS = 2 * K * H * S + 2 * H * H * M
+
+F32 = mybir.dt.float32
+BF16 = mybir.dt.bfloat16
+I32 = mybir.dt.int32
+U32 = mybir.dt.uint32
+U16 = mybir.dt.uint16
+U8 = mybir.dt.uint8
+FP8X4 = mybir.dt.float8_e4m3fn_x4
+FP4X4 = mybir.dt.float4_e2m1fn_x4
+ALU = mybir.AluOpType
+ACT = mybir.ActivationFunctionType
+
+P = 128
+BANK = 512
+TILES = H // P
+TURN = 2.0 * math.pi
+TURN_OFFSET = 1024.0
+
+
+def tile_rows(matrix, u):
+    b, t = divmod(u, 4)
+    return matrix.rearrange("(b g t i) c -> b t g i c", b=2, g=16, t=4)[b, t]
+
+
+def tile_list_weave_fault_map_kernel(
+    tc, tab_words, tab_scales, offs, w4_words, w4_scales, pattern, gain, pos1, light, w2, skip, wgo, out
+):
+    nc = tc.nc
+    with ExitStack() as ctx:
+        keep = ctx.enter_context(tc.tile_pool(name="keep", bufs=1))
+        two = ctx.enter_context(tc.tile_pool(name="two", bufs=2))
+        three = ctx.enter_context(tc.tile_pool(name="three", bufs=3))
+        psum = ctx.enter_context(tc.psum_pool(name="psum", bufs=7))
+        psum1 = ctx.enter_context(tc.psum_pool(name="psum1", bufs=1))
+
+        idx = keep.tile([P, S // 16], U16, name="idx")
+        p1 = keep.tile([P, M // 16], U16, name="p1")
+        w4_s_raw = keep.tile([32, H // 4], I32, name="w4_s_raw", align_bytes=64)
+        v_s = keep.tile([P, S], U8, name="v_s", align_bytes=64)
+        scale_rows = keep.tile([32, 2, S // 4], I32, name="scale_rows", align_bytes=64)
+        planes = keep.tile([P, 2, 2, S // 4], I32, name="planes", align_bytes=64)
+        tab_w = [keep.tile([P, T], I32, name=f"tab_w{a}", align_bytes=64) for a in range(2)]
+        w4_w_raw = keep.tile([P, 2, H // 2], I32, name="w4_w_raw", align_bytes=64)
+        ident = keep.tile([P, P], F32, name="ident")
+        rows = keep.tile([P, 2, P], F32, name="rows")
+        factors = keep.tile([P, 2, TILES], F32, name="factors")
+
+        with tc.tile_pool(name="early", bufs=1) as early:
+            tab_s = early.tile([P, T // 4], I32, name="tab_s", align_bytes=64)
+            nc.gpsimd.memset(rows[:], 0.0)
+            nc.sync.dma_start(idx[:], offs)
+            nc.sync.dma_start(tab_s[0:32, :], tab_scales.bitcast(I32).rearrange("a r w -> r a w"))
+            nc.sync.dma_start(w4_s_raw[:], w4_scales.bitcast(I32).rearrange("a r w -> r a w"))
+            nc.sync.dma_start(p1[:], pos1)
+            nc.sync.dma_start(tab_w[0][:], tab_words[0].rearrange("p t i -> p (t i)").bitcast(I32))
+            nc.sync.dma_start(w4_w_raw[:], w4_words.bitcast(I32).rearrange("a p w -> p a w"))
+            nc.sync.dma_start(tab_w[1][:], tab_words[1].rearrange("p t i -> p (t i)").bitcast(I32))
+            for j, vec in enumerate((gain, skip)):
+                nc.sync.dma_start(
+                    rows[4 * j : 4 * j + 4].rearrange("t b (g i) -> t (b g) i", i=8),
+                    vec.rearrange("(bg t i) -> t bg i", t=4, i=8),
+                )
+            nc.vector.memset(tab_s[32:64, :], 0)
+            nc.vector.memset(tab_s[64:128, :], 0)
+            nc.vector.memset(planes[:], 0)
+            make_identity(nc, ident[:])
+            nc.vector.tensor_copy(
+                scale_rows[:, 1, :].rearrange("p (b t g w) -> p b t g w", b=2, t=4, g=16),
+                w4_s_raw[:].rearrange("p (b g t w) -> p b t g w", b=2, g=16, t=4),
+            )
+            nc.vector.tensor_copy(v_s[:], tab_s[:].bitcast(U8).indirect(idx[:]))
+        nc.vector.tensor_copy(scale_rows[:, 0, :], v_s[:].bitcast(I32)[0:32, :])
+        for q in range(4):
+            nc.sync.dma_start(planes[32 * q : 32 * q + 4], scale_rows[8 * q : 8 * q + 8])
+        v_scales = [planes[:, a, 0, :].bitcast(U8) for a in range(2)]
+        w4_planes = [planes[:, a, 1, :].bitcast(U8) for a in range(2)]
+
+        late = ctx.enter_context(tc.tile_pool(name="late", bufs=1))
+        h = [late.tile([P, S], F32, name=f"h{u}") for u in range(TILES)]
+        light_sb = [late.tile([P, 4, M], F32, name=f"light{b}") for b in range(2)]
+        w2_sb = [late.tile([P, 4, H], F32, name=f"w2_{b}") for b in range(2)]
+        wgo_sb = late.tile([P, 4, M], F32, name="wgo_sb")
+
+        for u in range(4):
+            nc.sync.dma_start(h[u][:], tile_rows(pattern, u))
+        for t in range(4):
+            nc.sync.dma_start(light_sb[0][:, t, :], tile_rows(light, t))
+        for u in range(4, TILES):
+            nc.sync.dma_start(h[u][:], tile_rows(pattern, u))
+        for u in range(TILES):
+            nc.sync.dma_start(w2_sb[u // 4][:, u % 4, :], tile_rows(w2, u))
+        for t in range(4):
+            nc.sync.dma_start(light_sb[1][:, t, :], tile_rows(light, 4 + t))
+        wgo_by_tile = wgo.rearrange("(g t i) m -> t g i m", g=4, t=4)
+        for t in range(4):
+            nc.sync.dma_start(wgo_sb[0:32, t, :], wgo_by_tile[t])
+        nc.sync.dma_start(wgo_sb[32:64], wgo_sb[0:32])
+        nc.sync.dma_start(wgo_sb[64:128], wgo_sb[0:64])
+
+        turned = psum1.tile([P, 2, P], F32, name="turned")
+        for b in range(2):
+            nc.tensor.transpose(turned[:, b, :], rows[:, b, :], ident[:])
+        nc.scalar.copy(
+            factors[:].rearrange("p j (b t) -> p b j t", b=2),
+            turned[:, :, 0:8].rearrange("p b (j t) -> p b j t", j=2),
+        )
+
+        v_w = [[keep.tile([P, BANK], U32, name=f"v_w{a}{half}", align_bytes=64) for half in range(2)] for a in range(2)]
+        w4_w = keep.tile([P, H], I32, name="w4_w", align_bytes=64)
+
+        def gather_words(a, half):
+            cols = BANK // 16
+            nc.vector.tensor_copy(
+                v_w[a][half][:], tab_w[a][:].bitcast(U32).indirect(idx[:, half * cols : (half + 1) * cols])
+            )
+
+        gather_words(0, 0)
+        gather_words(0, 1)
+        nc.vector.tensor_copy(
+            w4_w[:].rearrange("p (ab t g w) -> p ab t g w", ab=4, t=4, g=16),
+            w4_w_raw[:].rearrange("p a (b g t w) -> p (a b) t g w", b=2, g=16, t=4),
+        )
+        gather_words(1, 0)
+        gather_words(1, 1)
+        w4_codes = w4_w[:].bitcast(U8)
+
+        picked = [keep.tile([P, 4, M], F32, name=f"picked{b}") for b in range(2)]
+        x_codes = [keep.tile([P, M], U32, name=f"x_codes{b}", align_bytes=64) for b in range(2)]
+        x_scales = [keep.tile([P, M], U8, name=f"x_scales{b}", align_bytes=64) for b in range(2)]
+        angle = {}
+        w2_q = {}
+        page = {}
+
+        def first_product(u):
+            turns = two.tile([P, S], I32, name="turns")
+            banks = []
+            for half in range(2):
+                z = psum.tile([P, BANK], F32, name="bank")
+                for a in range(2):
+                    col = (a * TILES + u) * P
+                    nc.tensor.matmul_mx(
+                        out=z[:],
+                        lhsT=w4_codes[:, 2 * col : 2 * (col + P)].bitcast(FP4X4),
+                        lhsT_scale=w4_planes[a][:, u * P : (u + 1) * P],
+                        rhs=v_w[a][half][:].bitcast(FP8X4),
+                        rhs_scale=v_scales[a][:, half * BANK : (half + 1) * BANK],
+                        start=(a == 0),
+                        stop=(a == 1),
+                    )
+                banks.append(z)
+            d = three.tile([P, S], F32, name="d")
+            halves = [slice(half * BANK, (half + 1) * BANK) for half in range(2)]
+            if u == 0:
+                for z, cols in zip(banks, halves):
+                    nc.vector.tensor_scalar(turns[:, cols], z[:], 1.0 / TURN, None, ALU.mult)
+                for z, cols in zip(banks, halves):
+                    nc.vector.scalar_tensor_tensor(d[:, cols], turns[:, cols], -TURN, z[:], ALU.mult, ALU.add)
+            else:
+                shifted = turns[:].bitcast(U32)
+                for z, cols in zip(banks, halves):
+                    nc.scalar.activation(shifted[:, cols], z[:], ACT.Copy, bias=TURN_OFFSET, scale=1.0 / TURN)
+                nc.scalar.activation(d[:], shifted, ACT.Copy, bias=TURN * TURN_OFFSET, scale=-TURN)
+                for z, cols in zip(banks, halves):
+                    nc.vector.tensor_tensor(d[:, cols], z[:], d[:, cols], ALU.add)
+            angle[u] = d
+
+        def features(u):
+            wave = two.tile([P, S], F32, name="wave")
+            nc.scalar.activation(wave[:], angle[u][:], ACT.Sin)
+            nc.vector.scalar_tensor_tensor(h[u][:], wave[:], factors[:, 0, u : u + 1], h[u][:], ALU.mult, ALU.mult)
+
+        def pick(u):
+            b, t = divmod(u, 4)
+            nc.vector.tensor_copy(picked[b][:, t, :], h[u][:].indirect(p1[:]))
+
+        def light_and_round(b):
+            x = two.tile([P, M, 4], BF16, name="x", align_bytes=64)
+            nc.vector.tensor_tensor(
+                x[:].rearrange("p (c i) t -> p c t i", i=4),
+                picked[b][:].rearrange("p t (c i) -> p c t i", i=4),
+                light_sb[b][:].rearrange("p t (c i) -> p c t i", i=4),
+                ALU.mult,
+            )
+            return x
+
+        def quantize_x(b, x):
+            nc.vector.quantize_mx(
+                out=x_codes[b][:].bitcast(FP8X4), scales=x_scales[b][:], in_=x[:].rearrange("p m t -> p (m t)")
+            )
+
+        def prepare_w2(u):
+            bo, to = divmod(u, 4)
+            grouped = three.tile([P, 2, P, 4], BF16, name="grouped", align_bytes=64)
+            for b in range(2):
+                source = w2_sb[b][:, :, BANK * bo : BANK * (bo + 1)]
+                nc.scalar.copy(
+                    grouped[:, b].rearrange("p (g e i) t -> p g e t i", e=2, i=4),
+                    source.rearrange("p t (g o e i) -> p o g e t i", o=4, e=2, i=4)[:, to],
+                )
+            codes = three.tile([P, 2 * P], U32, name="w2_codes", align_bytes=64)
+            scales = three.tile([P, 2 * P], U8, name="w2_scales", align_bytes=64)
+            nc.vector.quantize_mx(
+                out=codes[:].bitcast(FP8X4), scales=scales[:], in_=grouped[:].rearrange("p b n t -> p (b n t)")
+            )
+            w2_q[u] = (codes, scales)
+
+        def fill_page(u):
+            page[u] = three.tile([P, S], F32, name="page")
+            nc.scalar.activation(page[u][:], h[u][:], ACT.Copy, scale=factors[:, 1, u : u + 1])
+
+        def second_product(u):
+            bo, to = divmod(u, 4)
+            codes, scales = w2_q[u]
+            y = psum.tile([P, BANK], F32, name="bank")
+            for b in range(2):
+                nc.tensor.matmul_mx(
+                    out=y[:],
+                    lhsT=codes[:, b * P : (b + 1) * P].bitcast(FP8X4),
+                    lhsT_scale=scales[:, b * P : (b + 1) * P],
+                    rhs=x_codes[b][:].bitcast(FP8X4),
+                    rhs_scale=x_scales[b][:],
+                    start=(b == 0),
+                    stop=(b == 1),
+                )
+            larger = two.tile([P, M], F32, name="larger")
+            nc.vector.scalar_tensor_tensor(
+                larger[:], picked[bo][:, to, :], factors[:, 1, u : u + 1], y[:], ALU.mult, ALU.max
+            )
+            return larger
+
+        def replace_and_store(u, larger):
+            nc.vector.tensor_tensor(page[u][:].indirect(p1[:]), larger[:], wgo_sb[:, u % 4, :], ALU.mult)
+            nc.sync.dma_start(tile_rows(out, u), page[u][:])
+
+        rounded = {}
+        for step in range(TILES + 2):
+            if step < TILES:
+                first_product(step)
+            if 1 <= step <= TILES:
+                features(step - 1)
+            if step >= 2:
+                pick(step - 2)
+            if step == 5:
+                rounded[0] = light_and_round(0)
+            if step == 6:
+                quantize_x(0, rounded[0])
+        prepare_w2(0)
+        fill_page(0)
+        rounded[1] = light_and_round(1)
+        prepare_w2(1)
+        quantize_x(1, rounded[1])
+        larger = {0: second_product(0)}
+        for u in range(TILES):
+            if u + 1 < TILES:
+                fill_page(u + 1)
+                larger[u + 1] = second_product(u + 1)
+            if u + 2 < TILES:
+                prepare_w2(u + 2)
+            replace_and_store(u, larger[u])

@@ -156,7 +156,7 @@ def tile_list_weave_fault_map_kernel(
                         stop=(a == 1),
                     )
                 banks.append(z)
-            d = three.tile([P, S], F32, name="d")
+            d = three.tile([P, S], F32, name="d", bufs=4)
             halves = [slice(half * BANK, (half + 1) * BANK) for half in range(2)]
             if u == 0:
                 for z, cols in zip(banks, halves):
@@ -173,7 +173,7 @@ def tile_list_weave_fault_map_kernel(
             angle[u] = d
 
         def features(u):
-            wave = two.tile([P, S], F32, name="wave")
+            wave = three.tile([P, S], F32, name="wave")
             nc.scalar.activation(wave[:], angle[u][:], ACT.Sin)
             nc.vector.scalar_tensor_tensor(h[u][:], wave[:], factors[:, 0, u : u + 1], h[u][:], ALU.mult, ALU.mult)
 
@@ -184,9 +184,9 @@ def tile_list_weave_fault_map_kernel(
         def light_and_round(b):
             x = two.tile([P, M, 4], BF16, name="x", align_bytes=64)
             nc.vector.tensor_tensor(
-                x[:].rearrange("p (c i) t -> p c t i", i=4),
-                picked[b][:].rearrange("p t (c i) -> p c t i", i=4),
-                light_sb[b][:].rearrange("p t (c i) -> p c t i", i=4),
+                x[:].rearrange("p (c i) t -> p c t i", i=2),
+                picked[b][:].rearrange("p t (c i) -> p c t i", i=2),
+                light_sb[b][:].rearrange("p t (c i) -> p c t i", i=2),
                 ALU.mult,
             )
             return x
@@ -202,8 +202,8 @@ def tile_list_weave_fault_map_kernel(
             for b in range(2):
                 source = w2_sb[b][:, :, BANK * bo : BANK * (bo + 1)]
                 nc.scalar.copy(
-                    grouped[:, b].rearrange("p (g e i) t -> p g e t i", e=2, i=4),
-                    source.rearrange("p t (g o e i) -> p o g e t i", o=4, e=2, i=4)[:, to],
+                    grouped[:, b].rearrange("p (g e i) t -> p g e t i", e=4, i=2),
+                    source.rearrange("p t (g o e i) -> p o g e t i", o=4, e=4, i=2)[:, to],
                 )
             codes = three.tile([P, 2 * P], U32, name="w2_codes", align_bytes=64)
             scales = three.tile([P, 2 * P], U8, name="w2_scales", align_bytes=64)
@@ -230,7 +230,7 @@ def tile_list_weave_fault_map_kernel(
                     start=(b == 0),
                     stop=(b == 1),
                 )
-            larger = two.tile([P, M], F32, name="larger")
+            larger = three.tile([P, M], F32, name="larger")
             nc.vector.scalar_tensor_tensor(
                 larger[:], picked[bo][:, to, :], factors[:, 1, u : u + 1], y[:], ALU.mult, ALU.max
             )

@@ -2,7 +2,6 @@ import math
 from contextlib import ExitStack
 
 import concourse.mybir as mybir
-from concourse.masks import make_identity
 
 K, H, T, S, M = 1024, 1024, 2048, 1024, 512
 FLOPS = 2 * K * H * S + 2 * H * H * M
@@ -27,7 +26,7 @@ TURN_OFFSET = 1024.0
 
 def tile_rows(matrix, u):
     b, t = divmod(u, 4)
-    return matrix.rearrange("(b g t i) c -> b t g i c", b=2, g=16, t=4)[b, t]
+    return matrix.rearrange("(b p t) c -> b t p c", b=2, t=4)[b, t]
 
 
 def tile_list_weave_fault_map_kernel(
@@ -38,46 +37,40 @@ def tile_list_weave_fault_map_kernel(
         keep = ctx.enter_context(tc.tile_pool(name="keep", bufs=1))
         two = ctx.enter_context(tc.tile_pool(name="two", bufs=2))
         three = ctx.enter_context(tc.tile_pool(name="three", bufs=3))
-        psum = ctx.enter_context(tc.psum_pool(name="psum", bufs=7))
-        psum1 = ctx.enter_context(tc.psum_pool(name="psum1", bufs=1))
+        psum = ctx.enter_context(tc.psum_pool(name="psum", bufs=8))
 
         idx = keep.tile([P, S // 16], U16, name="idx")
         p1 = keep.tile([P, M // 16], U16, name="p1")
-        w4_s_raw = keep.tile([32, H // 4], I32, name="w4_s_raw", align_bytes=64)
+        w4_s_raw = keep.tile([P, H // 4], I32, name="w4_s_raw", align_bytes=64)
         v_s = keep.tile([P, S], U8, name="v_s", align_bytes=64)
-        scale_rows = keep.tile([32, 2, S // 4], I32, name="scale_rows", align_bytes=64)
+        scale_rows = keep.tile([P, 2, S // 4], I32, name="scale_rows", align_bytes=64)
         planes = keep.tile([P, 2, 2, S // 4], I32, name="planes", align_bytes=64)
         tab_w = [keep.tile([P, T], I32, name=f"tab_w{a}", align_bytes=64) for a in range(2)]
         w4_w_raw = keep.tile([P, 2, H // 2], I32, name="w4_w_raw", align_bytes=64)
-        ident = keep.tile([P, P], F32, name="ident")
-        rows = keep.tile([P, 2, P], F32, name="rows")
-        factors = keep.tile([P, 2, TILES], F32, name="factors")
+        gains = keep.tile([P, 2, 4], F32, name="gains")
+        skips = keep.tile([P, 2, 4], F32, name="skips")
 
         with tc.tile_pool(name="early", bufs=1) as early:
             tab_s = early.tile([P, T // 4], I32, name="tab_s", align_bytes=64)
-            nc.gpsimd.memset(rows[:], 0.0)
             nc.sync.dma_start(idx[:], offs)
             nc.sync.dma_start(tab_s[0:32, :], tab_scales.bitcast(I32).rearrange("a r w -> r a w"))
-            nc.sync.dma_start(w4_s_raw[:], w4_scales.bitcast(I32).rearrange("a r w -> r a w"))
+            nc.sync.dma_start(w4_s_raw[0:32, :], w4_scales.bitcast(I32).rearrange("a r w -> r a w"))
             nc.sync.dma_start(p1[:], pos1)
             nc.sync.dma_start(tab_w[0][:], tab_words[0].rearrange("p t i -> p (t i)").bitcast(I32))
             nc.sync.dma_start(w4_w_raw[:], w4_words.bitcast(I32).rearrange("a p w -> p a w"))
             nc.sync.dma_start(tab_w[1][:], tab_words[1].rearrange("p t i -> p (t i)").bitcast(I32))
-            for j, vec in enumerate((gain, skip)):
-                nc.sync.dma_start(
-                    rows[4 * j : 4 * j + 4].rearrange("t b (g i) -> t (b g) i", i=8),
-                    vec.rearrange("(bg t i) -> t bg i", t=4, i=8),
-                )
-            nc.vector.memset(tab_s[32:64, :], 0)
-            nc.vector.memset(tab_s[64:128, :], 0)
+            nc.sync.dma_start(gains[:], gain.rearrange("(b p t) -> p b t", b=2, t=4))
+            nc.sync.dma_start(skips[:], skip.rearrange("(b p t) -> p b t", b=2, t=4))
+            for tile in (tab_s, w4_s_raw):
+                nc.vector.memset(tile[32:64, :], 0)
+                nc.vector.memset(tile[64:128, :], 0)
             nc.vector.memset(planes[:], 0)
-            make_identity(nc, ident[:])
             nc.vector.tensor_copy(
-                scale_rows[:, 1, :].rearrange("p (b t g w) -> p b t g w", b=2, t=4, g=16),
-                w4_s_raw[:].rearrange("p (b g t w) -> p b t g w", b=2, g=16, t=4),
+                scale_rows[:, 1, :].bitcast(U8).rearrange("p (b t q) -> p b t q", b=2, t=4),
+                w4_s_raw[:].bitcast(U8).rearrange("p (b q t) -> p b t q", b=2, t=4),
             )
             nc.vector.tensor_copy(v_s[:], tab_s[:].bitcast(U8).indirect(idx[:]))
-        nc.vector.tensor_copy(scale_rows[:, 0, :], v_s[:].bitcast(I32)[0:32, :])
+        nc.vector.tensor_copy(scale_rows[0:32, 0, :], v_s[:].bitcast(I32)[0:32, :])
         for q in range(4):
             nc.sync.dma_start(planes[32 * q : 32 * q + 4], scale_rows[8 * q : 8 * q + 8])
         v_scales = [planes[:, a, 0, :].bitcast(U8) for a in range(2)]
@@ -86,32 +79,23 @@ def tile_list_weave_fault_map_kernel(
         late = ctx.enter_context(tc.tile_pool(name="late", bufs=1))
         h = [late.tile([P, S], F32, name=f"h{u}") for u in range(TILES)]
         light_sb = [late.tile([P, 4, M], F32, name=f"light{b}") for b in range(2)]
-        w2_sb = [late.tile([P, 4, H], F32, name=f"w2_{b}") for b in range(2)]
+        w2_sb = [[late.tile([P, 4, BANK], F32, name=f"w2_{b}{bo}") for bo in range(2)] for b in range(2)]
         wgo_sb = late.tile([P, 4, M], F32, name="wgo_sb")
+        light_by_pass = light.rearrange("(b p t) m -> b p t m", b=2, t=4)
+        w2_by_pass = w2.rearrange("(b p t) n -> b p t n", b=2, t=4)
 
         for u in range(4):
             nc.sync.dma_start(h[u][:], tile_rows(pattern, u))
-        for t in range(4):
-            nc.sync.dma_start(light_sb[0][:, t, :], tile_rows(light, t))
+        nc.sync.dma_start(light_sb[0][:], light_by_pass[0])
         for u in range(4, TILES):
             nc.sync.dma_start(h[u][:], tile_rows(pattern, u))
-        for u in range(TILES):
-            nc.sync.dma_start(w2_sb[u // 4][:, u % 4, :], tile_rows(w2, u))
-        for t in range(4):
-            nc.sync.dma_start(light_sb[1][:, t, :], tile_rows(light, 4 + t))
-        wgo_by_tile = wgo.rearrange("(g t i) m -> t g i m", g=4, t=4)
-        for t in range(4):
-            nc.sync.dma_start(wgo_sb[0:32, t, :], wgo_by_tile[t])
-        nc.sync.dma_start(wgo_sb[32:64], wgo_sb[0:32])
-        nc.sync.dma_start(wgo_sb[64:128], wgo_sb[0:64])
-
-        turned = psum1.tile([P, 2, P], F32, name="turned")
+        nc.sync.dma_start(light_sb[1][:], light_by_pass[1])
         for b in range(2):
-            nc.tensor.transpose(turned[:, b, :], rows[:, b, :], ident[:])
-        nc.scalar.copy(
-            factors[:].rearrange("p j (b t) -> p b j t", b=2),
-            turned[:, :, 0:8].rearrange("p b (j t) -> p b j t", j=2),
-        )
+            nc.sync.dma_start(w2_sb[b][0][:], w2_by_pass[b][:, :, 0:BANK])
+        for q in range(4):
+            nc.sync.dma_start(wgo_sb[32 * q : 32 * (q + 1)], wgo.rearrange("(p t) m -> p t m", t=4))
+        for b in range(2):
+            nc.sync.dma_start(w2_sb[b][1][:], w2_by_pass[b][:, :, BANK:H])
 
         v_w = [[keep.tile([P, BANK], U32, name=f"v_w{a}{half}", align_bytes=64) for half in range(2)] for a in range(2)]
         w4_w = keep.tile([P, H], I32, name="w4_w", align_bytes=64)
@@ -125,8 +109,8 @@ def tile_list_weave_fault_map_kernel(
         gather_words(0, 0)
         gather_words(0, 1)
         nc.vector.tensor_copy(
-            w4_w[:].rearrange("p (ab t g w) -> p ab t g w", ab=4, t=4, g=16),
-            w4_w_raw[:].rearrange("p a (b g t w) -> p (a b) t g w", b=2, g=16, t=4),
+            w4_w[:].bitcast(U16).rearrange("p (ab t q) -> p ab t q", ab=4, t=4),
+            w4_w_raw[:].bitcast(U16).rearrange("p a (b q t) -> p (a b) t q", b=2, t=4),
         )
         gather_words(1, 0)
         gather_words(1, 1)
@@ -137,6 +121,7 @@ def tile_list_weave_fault_map_kernel(
         x_scales = [keep.tile([P, M], U8, name=f"x_scales{b}", align_bytes=64) for b in range(2)]
         angle = {}
         w2_q = {}
+        w2_rounded = {}
         page = {}
 
         def first_product(u):
@@ -175,7 +160,7 @@ def tile_list_weave_fault_map_kernel(
         def features(u):
             wave = three.tile([P, S], F32, name="wave")
             nc.scalar.activation(wave[:], angle[u][:], ACT.Sin)
-            nc.vector.scalar_tensor_tensor(h[u][:], wave[:], factors[:, 0, u : u + 1], h[u][:], ALU.mult, ALU.mult)
+            nc.vector.scalar_tensor_tensor(h[u][:], wave[:], gains[:, u // 4, u % 4 : u % 4 + 1], h[u][:], ALU.mult, ALU.mult)
 
         def pick(u):
             b, t = divmod(u, 4)
@@ -196,25 +181,29 @@ def tile_list_weave_fault_map_kernel(
                 out=x_codes[b][:].bitcast(FP8X4), scales=x_scales[b][:], in_=x[:].rearrange("p m t -> p (m t)")
             )
 
-        def prepare_w2(u):
-            bo, to = divmod(u, 4)
-            grouped = three.tile([P, 2, P, 4], BF16, name="grouped", align_bytes=64)
+        def round_w2(pair):
+            bo, first = divmod(2 * pair, 4)
+            grouped = two.tile([P, 2, 2, P, 4], BF16, name="grouped", align_bytes=64)
             for b in range(2):
-                source = w2_sb[b][:, :, BANK * bo : BANK * (bo + 1)]
                 nc.scalar.copy(
-                    grouped[:, b].rearrange("p (g e i) t -> p g e t i", e=4, i=2),
-                    source.rearrange("p t (g o e i) -> p o g e t i", o=4, e=4, i=2)[:, to],
+                    grouped[:, :, b].rearrange("p o q t -> p q t o"),
+                    w2_sb[b][bo][:].rearrange("p t (q o) -> p q t o", o=4)[:, :, :, first : first + 2],
                 )
-            codes = three.tile([P, 2 * P], U32, name="w2_codes", align_bytes=64)
-            scales = three.tile([P, 2 * P], U8, name="w2_scales", align_bytes=64)
+            w2_rounded[pair] = grouped
+
+        def quantize_w2(u):
+            codes = keep.tile([P, 2 * P], U32, name="w2_codes", align_bytes=64, bufs=4)
+            scales = keep.tile([P, 2 * P], U8, name="w2_scales", align_bytes=64, bufs=4)
             nc.vector.quantize_mx(
-                out=codes[:].bitcast(FP8X4), scales=scales[:], in_=grouped[:].rearrange("p b n t -> p (b n t)")
+                out=codes[:].bitcast(FP8X4),
+                scales=scales[:],
+                in_=w2_rounded[u // 2][:, u % 2].rearrange("p b n t -> p (b n t)"),
             )
             w2_q[u] = (codes, scales)
 
         def fill_page(u):
             page[u] = three.tile([P, S], F32, name="page")
-            nc.scalar.activation(page[u][:], h[u][:], ACT.Copy, scale=factors[:, 1, u : u + 1])
+            nc.scalar.activation(page[u][:], h[u][:], ACT.Copy, scale=skips[:, u // 4, u % 4 : u % 4 + 1])
 
         def second_product(u):
             bo, to = divmod(u, 4)
@@ -232,7 +221,7 @@ def tile_list_weave_fault_map_kernel(
                 )
             larger = three.tile([P, M], F32, name="larger")
             nc.vector.scalar_tensor_tensor(
-                larger[:], picked[bo][:, to, :], factors[:, 1, u : u + 1], y[:], ALU.mult, ALU.max
+                larger[:], picked[bo][:, to, :], skips[:, u // 4, u % 4 : u % 4 + 1], y[:], ALU.mult, ALU.max
             )
             return larger
 
@@ -252,16 +241,21 @@ def tile_list_weave_fault_map_kernel(
                 rounded[0] = light_and_round(0)
             if step == 6:
                 quantize_x(0, rounded[0])
-        prepare_w2(0)
+        round_w2(0)
         fill_page(0)
+        round_w2(1)
+        quantize_w2(0)
         rounded[1] = light_and_round(1)
-        prepare_w2(1)
+        quantize_w2(1)
         quantize_x(1, rounded[1])
+        quantize_w2(2)
         larger = {0: second_product(0)}
         for u in range(TILES):
+            if u % 2 == 0 and u + 4 < TILES:
+                round_w2(u // 2 + 2)
             if u + 1 < TILES:
                 fill_page(u + 1)
                 larger[u + 1] = second_product(u + 1)
-            if u + 2 < TILES:
-                prepare_w2(u + 2)
+            if u + 3 < TILES:
+                quantize_w2(u + 3)
             replace_and_store(u, larger[u])

@@ -22,6 +22,7 @@ BANK = 512
 TILES = H // P
 TURN = 2.0 * math.pi
 TURN_OFFSET = 1024.0
+VECTOR_REDUCED = (0, 1, 3)
 
 
 def tile_rows(matrix, u):
@@ -78,18 +79,18 @@ def tile_list_weave_fault_map_kernel(
 
         late = ctx.enter_context(tc.tile_pool(name="late", bufs=1))
         h = [late.tile([P, S], F32, name=f"h{u}") for u in range(TILES)]
-        light_sb = [late.tile([P, 4, M], F32, name=f"light{b}") for b in range(2)]
+        light_sb = late.tile([P, 4, 2, M], F32, name="light_sb")
         w2_sb = [[late.tile([P, 4, BANK], F32, name=f"w2_{b}{bo}") for bo in range(2)] for b in range(2)]
         wgo_sb = late.tile([P, 4, M], F32, name="wgo_sb")
         light_by_pass = light.rearrange("(b p t) m -> b p t m", b=2, t=4)
         w2_by_pass = w2.rearrange("(b p t) n -> b p t n", b=2, t=4)
 
-        for u in range(4):
+        nc.sync.dma_start(light_sb[:, :, 0, :], light_by_pass[0])
+        for u in range(2):
             nc.sync.dma_start(h[u][:], tile_rows(pattern, u))
-        nc.sync.dma_start(light_sb[0][:], light_by_pass[0])
-        for u in range(4, TILES):
+        nc.sync.dma_start(light_sb[:, :, 1, :], light_by_pass[1])
+        for u in range(2, TILES):
             nc.sync.dma_start(h[u][:], tile_rows(pattern, u))
-        nc.sync.dma_start(light_sb[1][:], light_by_pass[1])
         for b in range(2):
             nc.sync.dma_start(w2_sb[b][0][:], w2_by_pass[b][:, :, 0:BANK])
         for q in range(4):
@@ -116,10 +117,13 @@ def tile_list_weave_fault_map_kernel(
         gather_words(1, 1)
         w4_codes = w4_w[:].bitcast(U8)
 
-        picked = [keep.tile([P, 4, M], F32, name=f"picked{b}") for b in range(2)]
-        x_codes = [keep.tile([P, M], U32, name=f"x_codes{b}", align_bytes=64) for b in range(2)]
-        x_scales = [keep.tile([P, M], U8, name=f"x_scales{b}", align_bytes=64) for b in range(2)]
-        angle = {}
+        picked = keep.tile([P, 4, 2, M], F32, name="picked")
+        x_codes = keep.tile([P, 2 * M], U32, name="x_codes", align_bytes=64)
+        x_scales = keep.tile([P, 2 * M], U8, name="x_scales", align_bytes=64)
+        both = keep.tile([P, 2, 4], F32, name="both")
+        nc.vector.tensor_tensor(both[:], gains[:], skips[:], ALU.mult)
+        angles = [keep.tile([P, S], F32, name=f"angle{j}", align_bytes=64) for j in range(4)]
+        waves = [keep.tile([P, S], F32, name=f"wave{j}") for j in range(3)]
         w2_q = {}
         w2_rounded = {}
         page = {}
@@ -141,12 +145,11 @@ def tile_list_weave_fault_map_kernel(
                         stop=(a == 1),
                     )
                 banks.append(z)
-            d = three.tile([P, S], F32, name="d", bufs=4)
+            d = angles[u % 4]
             halves = [slice(half * BANK, (half + 1) * BANK) for half in range(2)]
-            if u == 0:
+            if u in VECTOR_REDUCED:
                 for z, cols in zip(banks, halves):
                     nc.vector.tensor_scalar(turns[:, cols], z[:], 1.0 / TURN, None, ALU.mult)
-                for z, cols in zip(banks, halves):
                     nc.vector.scalar_tensor_tensor(d[:, cols], turns[:, cols], -TURN, z[:], ALU.mult, ALU.add)
             else:
                 shifted = turns[:].bitcast(U32)
@@ -155,35 +158,42 @@ def tile_list_weave_fault_map_kernel(
                 nc.scalar.activation(d[:], shifted, ACT.Copy, bias=TURN * TURN_OFFSET, scale=-TURN)
                 for z, cols in zip(banks, halves):
                     nc.vector.tensor_tensor(d[:, cols], z[:], d[:, cols], ALU.add)
-            angle[u] = d
 
         def features(u):
-            wave = three.tile([P, S], F32, name="wave")
-            nc.scalar.activation(wave[:], angle[u][:], ACT.Sin)
-            nc.vector.scalar_tensor_tensor(h[u][:], wave[:], gains[:, u // 4, u % 4 : u % 4 + 1], h[u][:], ALU.mult, ALU.mult)
+            wave = waves[u % 3]
+            engine = nc.gpsimd if u < TILES - 1 else nc.vector
+            pieces = 2 if u == 0 else 1
+            for piece in range(pieces):
+                cols = slice(piece * S // pieces, (piece + 1) * S // pieces)
+                nc.scalar.activation(wave[:, cols], angles[u % 4][:, cols], ACT.Sin)
+                engine.tensor_tensor(h[u][:, cols], wave[:, cols], h[u][:, cols], ALU.mult)
+
+        def gain_on_light(u):
+            b, t = divmod(u, 4)
+            nc.scalar.activation(light_sb[:, t, b, :], light_sb[:, t, b, :], ACT.Copy, scale=gains[:, b, t : t + 1])
 
         def pick(u):
             b, t = divmod(u, 4)
-            nc.vector.tensor_copy(picked[b][:, t, :], h[u][:].indirect(p1[:]))
+            nc.vector.tensor_copy(picked[:, t, b, :], h[u][:].indirect(p1[:]))
 
-        def light_and_round(b):
-            x = two.tile([P, M, 4], BF16, name="x", align_bytes=64)
+        def light_and_round():
+            x = keep.tile([P, 2 * M, 4], BF16, name="x", align_bytes=64)
             nc.vector.tensor_tensor(
                 x[:].rearrange("p (c i) t -> p c t i", i=2),
-                picked[b][:].rearrange("p t (c i) -> p c t i", i=2),
-                light_sb[b][:].rearrange("p t (c i) -> p c t i", i=2),
+                picked[:].rearrange("p t b (c i) -> p (b c) t i", i=2),
+                light_sb[:].rearrange("p t b (c i) -> p (b c) t i", i=2),
                 ALU.mult,
             )
             return x
 
-        def quantize_x(b, x):
+        def quantize_x(x):
             nc.vector.quantize_mx(
-                out=x_codes[b][:].bitcast(FP8X4), scales=x_scales[b][:], in_=x[:].rearrange("p m t -> p (m t)")
+                out=x_codes[:].bitcast(FP8X4), scales=x_scales[:], in_=x[:].rearrange("p m t -> p (m t)")
             )
 
         def round_w2(pair):
             bo, first = divmod(2 * pair, 4)
-            grouped = two.tile([P, 2, 2, P, 4], BF16, name="grouped", align_bytes=64)
+            grouped = angles[3 - pair % 2][:].bitcast(BF16).rearrange("p (o b q t) -> p o b q t", o=2, b=2, t=4)
             for b in range(2):
                 nc.scalar.copy(
                     grouped[:, :, b].rearrange("p o q t -> p q t o"),
@@ -202,8 +212,8 @@ def tile_list_weave_fault_map_kernel(
             w2_q[u] = (codes, scales)
 
         def fill_page(u):
-            page[u] = three.tile([P, S], F32, name="page")
-            nc.scalar.activation(page[u][:], h[u][:], ACT.Copy, scale=skips[:, u // 4, u % 4 : u % 4 + 1])
+            page[u] = waves[(TILES + u) % 3]
+            nc.scalar.activation(page[u][:], h[u][:], ACT.Copy, scale=both[:, u // 4, u % 4 : u % 4 + 1])
 
         def second_product(u):
             bo, to = divmod(u, 4)
@@ -214,14 +224,14 @@ def tile_list_weave_fault_map_kernel(
                     out=y[:],
                     lhsT=codes[:, b * P : (b + 1) * P].bitcast(FP8X4),
                     lhsT_scale=scales[:, b * P : (b + 1) * P],
-                    rhs=x_codes[b][:].bitcast(FP8X4),
-                    rhs_scale=x_scales[b][:],
+                    rhs=x_codes[:, b * M : (b + 1) * M].bitcast(FP8X4),
+                    rhs_scale=x_scales[:, b * M : (b + 1) * M],
                     start=(b == 0),
                     stop=(b == 1),
                 )
             larger = three.tile([P, M], F32, name="larger")
             nc.vector.scalar_tensor_tensor(
-                larger[:], picked[bo][:, to, :], skips[:, u // 4, u % 4 : u % 4 + 1], y[:], ALU.mult, ALU.max
+                larger[:], picked[:, to, bo, :], both[:, u // 4, u % 4 : u % 4 + 1], y[:], ALU.mult, ALU.max
             )
             return larger
 
@@ -229,25 +239,22 @@ def tile_list_weave_fault_map_kernel(
             nc.vector.tensor_tensor(page[u][:].indirect(p1[:]), larger[:], wgo_sb[:, u % 4, :], ALU.mult)
             nc.sync.dma_start(tile_rows(out, u), page[u][:])
 
-        rounded = {}
-        for step in range(TILES + 2):
+        for step in range(TILES + 5):
             if step < TILES:
                 first_product(step)
             if 1 <= step <= TILES:
                 features(step - 1)
-            if step >= 2:
-                pick(step - 2)
-            if step == 5:
-                rounded[0] = light_and_round(0)
-            if step == 6:
-                quantize_x(0, rounded[0])
+            if step >= 5:
+                pick(step - 5)
+            if step >= 5:
+                gain_on_light(step - 5)
         round_w2(0)
         fill_page(0)
         round_w2(1)
         quantize_w2(0)
-        rounded[1] = light_and_round(1)
+        rounded = light_and_round()
         quantize_w2(1)
-        quantize_x(1, rounded[1])
+        quantize_x(rounded)
         quantize_w2(2)
         larger = {0: second_product(0)}
         for u in range(TILES):

import math
from contextlib import ExitStack

import concourse.mybir as mybir

K, H, T, S, M = 1024, 1024, 2048, 1024, 512
FLOPS = 2 * K * H * S + 2 * H * H * M

F32 = mybir.dt.float32
BF16 = mybir.dt.bfloat16
I32 = mybir.dt.int32
U32 = mybir.dt.uint32
U16 = mybir.dt.uint16
U8 = mybir.dt.uint8
FP8X4 = mybir.dt.float8_e4m3fn_x4
FP4X4 = mybir.dt.float4_e2m1fn_x4
ALU = mybir.AluOpType
ACT = mybir.ActivationFunctionType

P = 128
BANK = 512
TILES = H // P
TURN = 2.0 * math.pi
TURN_OFFSET = 1024.0
VECTOR_REDUCED = (0, 1, 3)


def tile_rows(matrix, u):
    b, t = divmod(u, 4)
    return matrix.rearrange("(b p t) c -> b t p c", b=2, t=4)[b, t]


def tile_list_weave_fault_map_kernel(
    tc, tab_words, tab_scales, offs, w4_words, w4_scales, pattern, gain, pos1, light, w2, skip, wgo, out
):
    nc = tc.nc
    with ExitStack() as ctx:
        keep = ctx.enter_context(tc.tile_pool(name="keep", bufs=1))
        two = ctx.enter_context(tc.tile_pool(name="two", bufs=2))
        three = ctx.enter_context(tc.tile_pool(name="three", bufs=3))
        psum = ctx.enter_context(tc.psum_pool(name="psum", bufs=8))

        idx = keep.tile([P, S // 16], U16, name="idx")
        p1 = keep.tile([P, M // 16], U16, name="p1")
        w4_s_raw = keep.tile([P, H // 4], I32, name="w4_s_raw", align_bytes=64)
        v_s = keep.tile([P, S], U8, name="v_s", align_bytes=64)
        scale_rows = keep.tile([P, 2, S // 4], I32, name="scale_rows", align_bytes=64)
        planes = keep.tile([P, 2, 2, S // 4], I32, name="planes", align_bytes=64)
        tab_w = [keep.tile([P, T], I32, name=f"tab_w{a}", align_bytes=64) for a in range(2)]
        w4_w_raw = keep.tile([P, 2, H // 2], I32, name="w4_w_raw", align_bytes=64)
        gains = keep.tile([P, 2, 4], F32, name="gains")
        skips = keep.tile([P, 2, 4], F32, name="skips")

        with tc.tile_pool(name="early", bufs=1) as early:
            tab_s = early.tile([P, T // 4], I32, name="tab_s", align_bytes=64)
            nc.sync.dma_start(idx[:], offs)
            nc.sync.dma_start(tab_s[0:32, :], tab_scales.bitcast(I32).rearrange("a r w -> r a w"))
            nc.sync.dma_start(w4_s_raw[0:32, :], w4_scales.bitcast(I32).rearrange("a r w -> r a w"))
            nc.sync.dma_start(p1[:], pos1)
            nc.sync.dma_start(tab_w[0][:], tab_words[0].rearrange("p t i -> p (t i)").bitcast(I32))
            nc.sync.dma_start(w4_w_raw[:], w4_words.bitcast(I32).rearrange("a p w -> p a w"))
            nc.sync.dma_start(tab_w[1][:], tab_words[1].rearrange("p t i -> p (t i)").bitcast(I32))
            nc.sync.dma_start(gains[:], gain.rearrange("(b p t) -> p b t", b=2, t=4))
            nc.sync.dma_start(skips[:], skip.rearrange("(b p t) -> p b t", b=2, t=4))
            for tile in (tab_s, w4_s_raw):
                nc.vector.memset(tile[32:64, :], 0)
                nc.vector.memset(tile[64:128, :], 0)
            nc.vector.memset(planes[:], 0)
            nc.vector.tensor_copy(
                scale_rows[:, 1, :].bitcast(U8).rearrange("p (b t q) -> p b t q", b=2, t=4),
                w4_s_raw[:].bitcast(U8).rearrange("p (b q t) -> p b t q", b=2, t=4),
            )
            nc.vector.tensor_copy(v_s[:], tab_s[:].bitcast(U8).indirect(idx[:]))
        nc.vector.tensor_copy(scale_rows[0:32, 0, :], v_s[:].bitcast(I32)[0:32, :])
        for q in range(4):
            nc.sync.dma_start(planes[32 * q : 32 * q + 4], scale_rows[8 * q : 8 * q + 8])
        v_scales = [planes[:, a, 0, :].bitcast(U8) for a in range(2)]
        w4_planes = [planes[:, a, 1, :].bitcast(U8) for a in range(2)]

        late = ctx.enter_context(tc.tile_pool(name="late", bufs=1))
        h = [late.tile([P, S], F32, name=f"h{u}") for u in range(TILES)]
        light_sb = late.tile([P, 4, 2, M], F32, name="light_sb")
        w2_sb = [[late.tile([P, 4, BANK], F32, name=f"w2_{b}{bo}") for bo in range(2)] for b in range(2)]
        wgo_sb = late.tile([P, 4, M], F32, name="wgo_sb")
        light_by_pass = light.rearrange("(b p t) m -> b p t m", b=2, t=4)
        w2_by_pass = w2.rearrange("(b p t) n -> b p t n", b=2, t=4)

        nc.sync.dma_start(light_sb[:, :, 0, :], light_by_pass[0])
        for u in range(2):
            nc.sync.dma_start(h[u][:], tile_rows(pattern, u))
        nc.sync.dma_start(light_sb[:, :, 1, :], light_by_pass[1])
        for u in range(2, TILES):
            nc.sync.dma_start(h[u][:], tile_rows(pattern, u))
        for b in range(2):
            nc.sync.dma_start(w2_sb[b][0][:], w2_by_pass[b][:, :, 0:BANK])
        for q in range(4):
            nc.sync.dma_start(wgo_sb[32 * q : 32 * (q + 1)], wgo.rearrange("(p t) m -> p t m", t=4))
        for b in range(2):
            nc.sync.dma_start(w2_sb[b][1][:], w2_by_pass[b][:, :, BANK:H])

        v_w = [[keep.tile([P, BANK], U32, name=f"v_w{a}{half}", align_bytes=64) for half in range(2)] for a in range(2)]
        w4_w = keep.tile([P, H], I32, name="w4_w", align_bytes=64)

        def gather_words(a, half):
            cols = BANK // 16
            nc.vector.tensor_copy(
                v_w[a][half][:], tab_w[a][:].bitcast(U32).indirect(idx[:, half * cols : (half + 1) * cols])
            )

        gather_words(0, 0)
        gather_words(0, 1)
        nc.vector.tensor_copy(
            w4_w[:].bitcast(U16).rearrange("p (ab t q) -> p ab t q", ab=4, t=4),
            w4_w_raw[:].bitcast(U16).rearrange("p a (b q t) -> p (a b) t q", b=2, t=4),
        )
        gather_words(1, 0)
        gather_words(1, 1)
        w4_codes = w4_w[:].bitcast(U8)

        picked = keep.tile([P, 4, 2, M], F32, name="picked")
        x_codes = keep.tile([P, 2 * M], U32, name="x_codes", align_bytes=64)
        x_scales = keep.tile([P, 2 * M], U8, name="x_scales", align_bytes=64)
        both = keep.tile([P, 2, 4], F32, name="both")
        nc.vector.tensor_tensor(both[:], gains[:], skips[:], ALU.mult)
        angles = [keep.tile([P, S], F32, name=f"angle{j}", align_bytes=64) for j in range(4)]
        waves = [keep.tile([P, S], F32, name=f"wave{j}") for j in range(3)]
        w2_q = {}
        w2_rounded = {}
        page = {}

        def first_product(u):
            turns = two.tile([P, S], I32, name="turns")
            banks = []
            for half in range(2):
                z = psum.tile([P, BANK], F32, name="bank")
                for a in range(2):
                    col = (a * TILES + u) * P
                    nc.tensor.matmul_mx(
                        out=z[:],
                        lhsT=w4_codes[:, 2 * col : 2 * (col + P)].bitcast(FP4X4),
                        lhsT_scale=w4_planes[a][:, u * P : (u + 1) * P],
                        rhs=v_w[a][half][:].bitcast(FP8X4),
                        rhs_scale=v_scales[a][:, half * BANK : (half + 1) * BANK],
                        start=(a == 0),
                        stop=(a == 1),
                    )
                banks.append(z)
            d = angles[u % 4]
            halves = [slice(half * BANK, (half + 1) * BANK) for half in range(2)]
            if u in VECTOR_REDUCED:
                for z, cols in zip(banks, halves):
                    nc.vector.tensor_scalar(turns[:, cols], z[:], 1.0 / TURN, None, ALU.mult)
                    nc.vector.scalar_tensor_tensor(d[:, cols], turns[:, cols], -TURN, z[:], ALU.mult, ALU.add)
            else:
                shifted = turns[:].bitcast(U32)
                for z, cols in zip(banks, halves):
                    nc.scalar.activation(shifted[:, cols], z[:], ACT.Copy, bias=TURN_OFFSET, scale=1.0 / TURN)
                nc.scalar.activation(d[:], shifted, ACT.Copy, bias=TURN * TURN_OFFSET, scale=-TURN)
                for z, cols in zip(banks, halves):
                    nc.vector.tensor_tensor(d[:, cols], z[:], d[:, cols], ALU.add)

        def features(u):
            wave = waves[u % 3]
            engine = nc.gpsimd if u < TILES - 1 else nc.vector
            pieces = 2 if u == 0 else 1
            for piece in range(pieces):
                cols = slice(piece * S // pieces, (piece + 1) * S // pieces)
                nc.scalar.activation(wave[:, cols], angles[u % 4][:, cols], ACT.Sin)
                engine.tensor_tensor(h[u][:, cols], wave[:, cols], h[u][:, cols], ALU.mult)

        def gain_on_light(u):
            b, t = divmod(u, 4)
            nc.scalar.activation(light_sb[:, t, b, :], light_sb[:, t, b, :], ACT.Copy, scale=gains[:, b, t : t + 1])

        def pick(u):
            b, t = divmod(u, 4)
            nc.vector.tensor_copy(picked[:, t, b, :], h[u][:].indirect(p1[:]))

        def light_and_round():
            x = keep.tile([P, 2 * M, 4], BF16, name="x", align_bytes=64)
            nc.vector.tensor_tensor(
                x[:].rearrange("p (c i) t -> p c t i", i=2),
                picked[:].rearrange("p t b (c i) -> p (b c) t i", i=2),
                light_sb[:].rearrange("p t b (c i) -> p (b c) t i", i=2),
                ALU.mult,
            )
            return x

        def quantize_x(x):
            nc.vector.quantize_mx(
                out=x_codes[:].bitcast(FP8X4), scales=x_scales[:], in_=x[:].rearrange("p m t -> p (m t)")
            )

        def round_w2(pair):
            bo, first = divmod(2 * pair, 4)
            grouped = angles[3 - pair % 2][:].bitcast(BF16).rearrange("p (o b q t) -> p o b q t", o=2, b=2, t=4)
            for b in range(2):
                nc.scalar.copy(
                    grouped[:, :, b].rearrange("p o q t -> p q t o"),
                    w2_sb[b][bo][:].rearrange("p t (q o) -> p q t o", o=4)[:, :, :, first : first + 2],
                )
            w2_rounded[pair] = grouped

        def quantize_w2(u):
            codes = keep.tile([P, 2 * P], U32, name="w2_codes", align_bytes=64, bufs=4)
            scales = keep.tile([P, 2 * P], U8, name="w2_scales", align_bytes=64, bufs=4)
            nc.vector.quantize_mx(
                out=codes[:].bitcast(FP8X4),
                scales=scales[:],
                in_=w2_rounded[u // 2][:, u % 2].rearrange("p b n t -> p (b n t)"),
            )
            w2_q[u] = (codes, scales)

        def fill_page(u):
            page[u] = waves[(TILES + u) % 3]
            nc.scalar.activation(page[u][:], h[u][:], ACT.Copy, scale=both[:, u // 4, u % 4 : u % 4 + 1])

        def second_product(u):
            bo, to = divmod(u, 4)
            codes, scales = w2_q[u]
            y = psum.tile([P, BANK], F32, name="bank")
            for b in range(2):
                nc.tensor.matmul_mx(
                    out=y[:],
                    lhsT=codes[:, b * P : (b + 1) * P].bitcast(FP8X4),
                    lhsT_scale=scales[:, b * P : (b + 1) * P],
                    rhs=x_codes[:, b * M : (b + 1) * M].bitcast(FP8X4),
                    rhs_scale=x_scales[:, b * M : (b + 1) * M],
                    start=(b == 0),
                    stop=(b == 1),
                )
            larger = three.tile([P, M], F32, name="larger")
            nc.vector.scalar_tensor_tensor(
                larger[:], picked[:, to, bo, :], both[:, u // 4, u % 4 : u % 4 + 1], y[:], ALU.mult, ALU.max
            )
            return larger

        def replace_and_store(u, larger):
            nc.vector.tensor_tensor(page[u][:].indirect(p1[:]), larger[:], wgo_sb[:, u % 4, :], ALU.mult)
            nc.sync.dma_start(tile_rows(out, u), page[u][:])

        for step in range(TILES + 5):
            if step < TILES:
                first_product(step)
            if 1 <= step <= TILES:
                features(step - 1)
            if step >= 5:
                pick(step - 5)
            if step >= 5:
                gain_on_light(step - 5)
        round_w2(0)
        fill_page(0)
        round_w2(1)
        quantize_w2(0)
        rounded = light_and_round()
        quantize_w2(1)
        quantize_x(rounded)
        quantize_w2(2)
        larger = {0: second_product(0)}
        for u in range(TILES):
            if u % 2 == 0 and u + 4 < TILES:
                round_w2(u // 2 + 2)
            if u + 1 < TILES:
                fill_page(u + 1)
                larger[u + 1] = second_product(u + 1)
            if u + 3 < TILES:
                quantize_w2(u + 3)
            replace_and_store(u, larger[u])
